import numpy as np
import ml_dtypes


def mxq(x, axis, fmt="e4m3"):
    dtype, down = {"e4m3": (ml_dtypes.float8_e4m3fn, 7), "e5m2": (ml_dtypes.float8_e5m2, 14)}[fmt]
    v = np.moveaxis(np.asarray(x, np.float32).astype(ml_dtypes.bfloat16).astype(np.float64), axis, -1)
    blocks = v.reshape(v.shape[:-1] + (-1, 32))
    amax = np.abs(blocks).max(-1, keepdims=True)
    byte = np.maximum(np.where(amax > 0, np.frexp(amax)[1] - 1 + 127, 0) - down, 1)
    scale = np.exp2(byte - 127.0)
    codes = (blocks / scale).astype(np.float32).astype(dtype).astype(np.float64)
    return np.moveaxis((codes * scale).reshape(v.shape), -1, axis)


WIDE = False


def mx_kscale(k):
    if not WIDE:
        return np.ones(k)
    levels = np.array([30, -30])
    if k % 512:
        return np.exp2(np.random.permutation(np.resize(levels, k // 32))).repeat(32)
    a = np.empty((k // 512, 16))
    for p in range(k // 512):
        a[p, :8] = np.random.permutation(np.resize(levels, 8))
        for g in range(8):
            far = levels[np.abs(levels - a[p, g]) >= 10]
            a[p, g + 8] = far[np.random.randint(len(far))]
    return np.exp2(a.ravel()).repeat(32)


def f64(x):
    return np.asarray(x).astype(np.float64)


def striped(idx):
    return np.tile(np.asarray(idx).reshape(-1, 16).T, (8, 1)).astype(np.uint16)


def unstriped(offs):
    return offs[:16].T.reshape(-1).astype(np.int64)


def striped8(idx):
    return np.asarray(idx).reshape(8, -1, 16).transpose(0, 2, 1).reshape(128, -1).astype(np.uint16)


def unstriped8(offs):
    return offs.reshape(8, 16, -1).transpose(0, 2, 1).reshape(8, -1).astype(np.int64)


def pick8(x, idx, run):
    r = np.arange(len(x))
    return x[r[:, None], idx[r % (8 * run) // run]]


E2M1 = np.array([0.0, 0.5, 1.0, 1.5, 2.0, 3.0, 4.0, 6.0, -0.0, -0.5, -1.0, -1.5, -2.0, -3.0, -4.0, -6.0])


def pack_weight(w, fmt):
    k, n = w.shape
    w = f64(np.asarray(w, np.float32).astype(ml_dtypes.bfloat16)).reshape(k // 32, 32, n)
    amax = np.abs(w).max(1)
    if fmt == "e4m3":
        byte = np.frexp(amax)[1] - 1 + 127 - 7
    else:
        mant, ex = np.frexp(amax / 6.0)
        byte = np.where(mant > 0.5, ex, ex - 1) + 127
    byte = np.clip(np.where(amax > 0, byte, 1), 1, 254)
    scaled = (w * np.exp2(127.0 - byte)[:, None, :]).reshape(k, n).astype(np.float32)
    by_word = np.ascontiguousarray(scaled.reshape(k // 512, 128, 4, n).transpose(0, 1, 3, 2))
    if fmt == "e4m3":
        words = by_word.astype(ml_dtypes.float8_e4m3fn).view(np.uint8)
    else:
        c = by_word.astype(ml_dtypes.float4_e2m1fn).view(np.uint8) & 0xF
        words = (c[..., 0::2] | (c[..., 1::2] << 4)).reshape(k // 512, 128, 2 * n)
    return np.ascontiguousarray(words), np.ascontiguousarray(byte.astype(np.uint8).reshape(k // 512, 16, n))


def unpack_weight(words, scales, fmt):
    g, _, n = scales.shape
    words = np.ascontiguousarray(words).reshape(g, 128, n, -1)
    if fmt == "e4m3":
        vals = words.view(ml_dtypes.float8_e4m3fn).astype(np.float64)
    else:
        nib = np.empty((g, 128, n, 4), np.uint8)
        nib[..., 0::2] = words & 0xF
        nib[..., 1::2] = words >> 4
        vals = E2M1[nib]
    vals = vals * np.repeat(np.exp2(scales.astype(np.float64) - 127.0), 8, axis=1)[..., None]
    return vals.transpose(0, 1, 3, 2).reshape(g * 512, n)


K, J, N, R, T, V = 512, 512, 256, 256, 1024, 1024


def setup_inputs():
    n = np.random.standard_normal
    idx = np.stack([np.random.permutation(T)[:J] for _ in range(8)])
    idx2 = np.random.permutation(V)[:J]
    fj = mx_kscale(J)
    fk = mx_kscale(K)
    drp = pack_weight(n((K, R)) * 1 / np.sqrt(K) / fk[:, None], "e2m1")
    return {
        "xf": (n((K, T))).astype(np.float32),
        "ra": (np.random.uniform(0.5, 1.5, (1, J)) * fj).astype(np.float32),
        "gt": (n((N, V)) * np.exp(0.5 * n((1, V)))).astype(np.float32),
        "rb": (np.random.uniform(0.5, 1.5, (1, J)) / fj).astype(np.float32),
        "cp": (np.random.uniform(0.4, 1.2, (N, 1))).astype(np.float32),
        "fkr": (np.random.uniform(0.5, 1.5, (1, K)) * fk).astype(np.float32),
        "dr_words": drp[0],
        "dr_scales": drp[1],
        "old": (12.0 * n((R, N))).astype(np.float32),
        "offs": striped8(idx),
        "offs2": striped(idx2),
    }


def reference(xf, ra, gt, rb, cp, fkr, dr_words, dr_scales, old, offs, offs2):
    idx = unstriped8(offs)
    idx2 = unstriped(offs2)
    dru = unpack_weight(dr_words, dr_scales, "e2m1")
    us = pick8(f64(xf), idx, 64) * f64(ra)
    ut = us.T
    uj = ut * f64(fkr)
    gs = np.minimum(f64(gt)[:, idx2], f64(cp)) * f64(rb)
    gj = gs.T
    ujq = mxq(uj, 0, "e5m2")
    gjq = mxq(gj, 0, "e5m2")
    w = ujq.T @ gjq
    wq = mxq(w, 0, "e5m2")
    v2 = dru.T @ wq
    y = 0.05 * np.maximum(v2, f64(old))
    return y

@@ -1,0 +1,211 @@
+from contextlib import ExitStack
+
+import concourse.mybir as mybir
+from concourse.masks import make_identity
+
+K, J, N, R, T, V = 512, 512, 256, 256, 1024, 1024
+FLOPS = 2 * J * K * N + 2 * K * R * N
+
+F32 = mybir.dt.float32
+BF16 = mybir.dt.bfloat16
+I32 = mybir.dt.int32
+U32 = mybir.dt.uint32
+U16 = mybir.dt.uint16
+U8 = mybir.dt.uint8
+E5M2X4 = mybir.dt.float8_e5m2_x4
+E2M1X4 = mybir.dt.float4_e2m1fn_x4
+ALU = mybir.AluOpType
+COPY = mybir.ActivationFunctionType.Copy
+
+P = 128
+PACK = 4
+PER_COLUMN = 16
+G_SHARE = (256, 128)
+X_SHARE = 128
+X_GROUPS = ((0, 1), (2,), (3,))
+OUT_SCALE = 0.05
+
+
+def tile_list_directions_headpicks_bounded_larger_kernel(
+    tc, xf, ra, gt, rb, cp, fkr, dr_words, dr_scales, old, offs, offs2, out
+):
+    nc = tc.nc
+    with ExitStack() as ctx:
+        lists = ctx.enter_context(tc.tile_pool(name="lists", bufs=1))
+        keep = ctx.enter_context(tc.tile_pool(name="keep", bufs=1))
+        shared = ctx.enter_context(tc.tile_pool(name="shared", bufs=1))
+        psum = ctx.enter_context(tc.psum_pool(name="psum", bufs=1))
+
+        g_list = lists.tile([P, J // PER_COLUMN], U16, name="g_list")
+        x_list = lists.tile([P, J // PER_COLUMN], U16, name="x_list")
+        g_rows = gt.rearrange("(p h) v -> h p v", h=2)
+        x_rows = xf.rearrange("(p i) t -> i p t", i=PACK)
+
+        def placed(shape, dtype, name, offset):
+            return shared.tile(shape, dtype, name=name, offset=offset, align_bytes=64)
+
+        def win_at(i):
+            return 4096 * i
+
+        def picks_at(i):
+            return 4096 * PACK + 2048 * (i + 2)
+
+        def rounded_at(i):
+            return 6144 * PACK + 2048 * (i + 2)
+
+        g_win = [keep.tile([P, V], F32, name=f"g_win{h}") for h in range(2)]
+        x_win = [placed([P, T], F32, f"x_win{i}", win_at(i)) for i in range(PACK)]
+        rb_col = keep.tile([P, PACK], F32, name="rb_col")
+        ra_col = keep.tile([P, PACK], F32, name="ra_col")
+        fkr_col = keep.tile([P, PACK], F32, name="fkr_col")
+        cp_col = keep.tile([P, 2], F32, name="cp_col")
+
+        nc.sync.dma_start(rb_col[:], rb.rearrange("o (q t) -> q (o t)", t=PACK))
+        nc.sync.dma_start(g_win[0][:], g_rows[0])
+        nc.sync.dma_start(g_list[:], offs2)
+        nc.sync.dma_start(cp_col[:], cp.rearrange("(p h) o -> p (h o)", h=2))
+        nc.sync.dma_start(ra_col[:], ra.rearrange("o (q t) -> q (o t)", t=PACK))
+        nc.sync.dma_start(x_list[:], offs)
+        nc.sync.dma_start(fkr_col[:], fkr.rearrange("o (p i) -> p (o i)", i=PACK))
+        nc.sync.dma_start(g_win[1][:], g_rows[1])
+        for i in range(PACK):
+            nc.sync.dma_start(x_win[i][:], x_rows[i])
+
+        old_sb = keep.tile([P, 2, N], F32, name="old_sb")
+        nc.sync.dma_start(old_sb[:], old.rearrange("(h p) n -> p h n", p=P))
+        dr_codes = keep.tile([P, 2 * R], U8, name="dr_codes", align_bytes=64)
+        nc.sync.dma_start(dr_codes[:].bitcast(I32), dr_words[0].bitcast(I32))
+        dr_plane = keep.tile([P, R], U8, name="dr_plane", align_bytes=64)
+        nc.gpsimd.memset(dr_plane[:].bitcast(I32), 0)
+        for quad in range(4):
+            nc.sync.dma_start(
+                dr_plane[32 * quad : 32 * quad + 4, :].bitcast(I32),
+                dr_scales[0, 4 * quad : 4 * quad + 4, :].bitcast(I32),
+            )
+
+        ident = keep.tile([P, P], F32, name="ident")
+        make_identity(nc, ident[:])
+
+        def spread(col, tag):
+            bank = psum.tile([P, PACK, P], F32, name=tag + "_spread", tag=tag)
+            for t in range(PACK):
+                nc.tensor.transpose(bank[:, t, :], col[:, t : t + 1].to_broadcast([P, P]), ident[:])
+            return bank
+
+        def by_slot(ap):
+            return ap.rearrange("p (q t) -> p q t", t=PACK)
+
+        def slots(bank, j0, j1):
+            return bank[:, :, j0 // PACK : j1 // PACK].rearrange("p t q -> p q t")
+
+        def listed(win, lst, j0, j1):
+            return win[:].indirect(lst[:, j0 // PER_COLUMN : j1 // PER_COLUMN])
+
+        rb_bank = spread(rb_col, "bank_a")
+        ra_bank = spread(ra_col, "bank_ra")
+        ra_row = keep.tile([P, X_SHARE], F32, name="ra_row")
+        nc.scalar.activation(by_slot(ra_row[:]), slots(ra_bank, 0, X_SHARE), COPY)
+
+        def turn(rounded, bank_part):
+            words = rounded[:].bitcast(F32)
+            for u in range(2):
+                nc.tensor.transpose(bank_part[:, u, :], words[:, u::2], ident[:])
+
+        def quantise(grouped, width, name, plane_at=None):
+            codes = keep.tile([P, width], U32, name=name + "_codes", align_bytes=64)
+            if plane_at is None:
+                plane = keep.tile([P, width], U8, name=name + "_plane", align_bytes=64)
+            else:
+                plane = placed([P, width], U8, name + "_plane", plane_at)
+            nc.vector.quantize_mx(codes[:].bitcast(E5M2X4), plane[:], grouped[:])
+            return codes, plane
+
+        g_bank = psum.tile([P, 2, 2, P], F32, name="g_bank", tag="bank_b")
+        for h in range(2):
+            share = G_SHARE[h]
+            on_v = keep.tile([P, share], F32, name=f"g_on_v{h}")
+            on_s = placed([P, J - share], F32, f"g_on_s{h}", picks_at(h - 2))
+            rounded = keep.tile([P, J], BF16, name=f"g_rounded{h}")
+            nc.scalar.activation(on_s[:], listed(g_win[h], g_list, share, J), COPY)
+            nc.vector.tensor_copy(on_v[:], listed(g_win[h], g_list, 0, share))
+            for part, j0, j1 in ((on_v, 0, share), (on_s, share, J)):
+                nc.vector.scalar_tensor_tensor(
+                    by_slot(rounded[:, j0:j1]), by_slot(part[:]), cp_col[:, h : h + 1],
+                    slots(rb_bank, j0, j1), ALU.min, ALU.mult,
+                )
+            turn(rounded, g_bank[:, h])
+
+        w_bank = [psum.tile([P, PACK, P], F32, name=f"w_bank{nh}", tag=f"bank_w{nh}") for nh in range(2)]
+        x_bank = [
+            psum.tile([P, len(group), 2, P], F32, name=f"x_bank{group[0]}", tag=f"bank_x{group[0]}")
+            for group in X_GROUPS
+        ]
+
+        def x_front(i, bank_part):
+            on_v = placed([P, X_SHARE], F32, f"x_on_v{i}", picks_at(i - 2))
+            on_s = placed([P, J - X_SHARE], F32, f"x_on_s{i}", picks_at(i))
+            rounded = placed([P, J], BF16, f"x_rounded{i}", rounded_at(i))
+            nc.scalar.activation(on_s[:], listed(x_win[i], x_list, X_SHARE, J), COPY)
+            nc.vector.tensor_tensor(on_v[:], listed(x_win[i], x_list, 0, X_SHARE), ra_row[:], ALU.mult)
+            nc.vector.tensor_scalar(rounded[:, :X_SHARE], on_v[:], fkr_col[:, i : i + 1], None, ALU.mult)
+            nc.vector.scalar_tensor_tensor(
+                by_slot(rounded[:, X_SHARE:]), by_slot(on_s[:]), fkr_col[:, i : i + 1],
+                slots(ra_bank, X_SHARE, J), ALU.mult, ALU.mult,
+            )
+            turn(rounded, bank_part)
+
+        for bank, group in zip(x_bank, X_GROUPS):
+            for place, i in enumerate(group):
+                x_front(i, bank[:, place])
+
+        g_grouped = placed([P, N * PACK], BF16, "g_grouped", win_at(1))
+        nc.scalar.copy(
+            g_grouped[:].bitcast(F32).rearrange("q (p c) -> q p c", c=4),
+            g_bank[:].rearrange("q h u p -> q p (h u)"),
+        )
+        g_codes, g_plane = quantise(g_grouped, N, "g", picks_at(PACK - 1))
+        for bank, group in zip(x_bank, X_GROUPS):
+            width = len(group) * P
+            grouped = placed([P, width * PACK], BF16, f"x_grouped{group[0]}", win_at(PACK - 1) + 1024 * group[0])
+            nc.scalar.copy(
+                grouped[:].bitcast(F32).rearrange("q (i p u) -> q i p u", u=2, p=P),
+                bank[:].rearrange("q i u p -> q i p u"),
+            )
+            codes, plane = quantise(grouped, width, f"x{group[0]}", picks_at(PACK - 1) + N + P * group[0])
+            for place, i in enumerate(group):
+                rows = slice(place * P, (place + 1) * P)
+                for nh in range(2):
+                    cols = slice(nh * P, (nh + 1) * P)
+                    nc.tensor.matmul_mx(
+                        w_bank[nh][:, i, :], lhsT=codes[:, rows].bitcast(E5M2X4), lhsT_scale=plane[:, rows],
+                        rhs=g_codes[:, cols].bitcast(E5M2X4), rhs_scale=g_plane[:, cols],
+                        start=True, stop=True,
+                    )
+
+        old_scaled = placed([P, 2, N], F32, "old_scaled", rounded_at(PACK - 1))
+        nc.scalar.activation(old_scaled[:], old_sb[:], COPY, scale=OUT_SCALE)
+        w_grouped = [keep.tile([P, P * PACK], BF16, name=f"w_grouped{nh}", align_bytes=64) for nh in range(2)]
+        for nh, copy_out in enumerate((nc.vector.tensor_copy, nc.scalar.copy)):
+            copy_out(
+                w_grouped[nh][:].rearrange("p (n i) -> p n i", i=PACK),
+                w_bank[nh][:].rearrange("p i n -> p n i"),
+            )
+        w_mx = [quantise(w_grouped[nh], P, f"w{nh}") for nh in range(2)]
+        out_rows = out.rearrange("(h p) n -> p h n", p=P)
+        for nh, tag in enumerate(("bank_a", "bank_b")):
+            codes, plane = w_mx[nh]
+            cols = slice(nh * P, (nh + 1) * P)
+            v_bank = psum.tile([P, 2, P], F32, name=f"v_bank{nh}", tag=tag)
+            for rh in range(2):
+                nc.tensor.matmul_mx(
+                    v_bank[:, rh, :],
+                    lhsT=dr_codes[:, 2 * rh * P : 2 * (rh + 1) * P].bitcast(E2M1X4),
+                    lhsT_scale=dr_plane[:, rh * P : (rh + 1) * P],
+                    rhs=codes[:].bitcast(E5M2X4), rhs_scale=plane[:],
+                    start=True, stop=True,
+                )
+            result = keep.tile([P, 2, P], F32, name=f"result{nh}")
+            nc.vector.scalar_tensor_tensor(
+                result[:], v_bank[:], OUT_SCALE, old_scaled[:, :, cols], ALU.mult, ALU.max
+            )
+            nc.sync.dma_start(out_rows[:, :, cols], result[:])

@@ -83,6 +83,10 @@ def tile_list_directions_headpicks_bounded_larger_kernel(
                 dr_scales[0, 4 * quad : 4 * quad + 4, :].bitcast(I32),
             )
 
+        warm = keep.tile([P, 2], F32, name="warm")
+        nc.vector.memset(warm[:, 0:1], 0.0)
+        nc.scalar.activation(warm[:, 1:2], warm[:, 0:1], COPY)
+
         ident = keep.tile([P, P], F32, name="ident")
         make_identity(nc, ident[:])
 

@@ -21,8 +21,7 @@ P = 128
 PACK = 4
 PER_COLUMN = 16
 G_SHARE = (256, 128)
-X_SHARE = 128
-X_GROUPS = ((0, 1), (2,), (3,))
+X_SHARE = (160, 160, 160, 192)
 OUT_SCALE = 0.05
 
 
@@ -107,8 +106,8 @@ def tile_list_directions_headpicks_bounded_larger_kernel(
 
         rb_bank = spread(rb_col, "bank_a")
         ra_bank = spread(ra_col, "bank_ra")
-        ra_row = keep.tile([P, X_SHARE], F32, name="ra_row")
-        nc.scalar.activation(by_slot(ra_row[:]), slots(ra_bank, 0, X_SHARE), COPY)
+        ra_row = keep.tile([P, max(X_SHARE)], F32, name="ra_row")
+        nc.scalar.activation(by_slot(ra_row[:]), slots(ra_bank, 0, max(X_SHARE)), COPY)
 
         def turn(rounded, bank_part):
             words = rounded[:].bitcast(F32)
@@ -140,51 +139,52 @@ def tile_list_directions_headpicks_bounded_larger_kernel(
             turn(rounded, g_bank[:, h])
 
         w_bank = [psum.tile([P, PACK, P], F32, name=f"w_bank{nh}", tag=f"bank_w{nh}") for nh in range(2)]
-        x_bank = [
-            psum.tile([P, len(group), 2, P], F32, name=f"x_bank{group[0]}", tag=f"bank_x{group[0]}")
-            for group in X_GROUPS
+        x_pair = psum.tile([P, 2, 2, P], F32, name="x_pair", tag="bank_x0")
+        x_bank = [x_pair[:, 0], x_pair[:, 1]] + [
+            psum.tile([P, 2, P], F32, name=f"x_bank{i}", tag=f"bank_x{i}")[:] for i in range(2, PACK)
         ]
 
-        def x_front(i, bank_part):
-            on_v = placed([P, X_SHARE], F32, f"x_on_v{i}", picks_at(i - 2))
-            on_s = placed([P, J - X_SHARE], F32, f"x_on_s{i}", picks_at(i))
+        for i in range(PACK):
+            share = X_SHARE[i]
+            on_v = placed([P, share], F32, f"x_on_v{i}", picks_at(i - 2))
+            on_s = placed([P, J - share], F32, f"x_on_s{i}", picks_at(i))
             rounded = placed([P, J], BF16, f"x_rounded{i}", rounded_at(i))
-            nc.scalar.activation(on_s[:], listed(x_win[i], x_list, X_SHARE, J), COPY)
-            nc.vector.tensor_tensor(on_v[:], listed(x_win[i], x_list, 0, X_SHARE), ra_row[:], ALU.mult)
-            nc.vector.tensor_scalar(rounded[:, :X_SHARE], on_v[:], fkr_col[:, i : i + 1], None, ALU.mult)
+            nc.scalar.activation(on_s[:], listed(x_win[i], x_list, share, J), COPY)
+            nc.vector.tensor_tensor(on_v[:], listed(x_win[i], x_list, 0, share), ra_row[:, :share], ALU.mult)
+            nc.vector.tensor_scalar(rounded[:, :share], on_v[:], fkr_col[:, i : i + 1], None, ALU.mult)
             nc.vector.scalar_tensor_tensor(
-                by_slot(rounded[:, X_SHARE:]), by_slot(on_s[:]), fkr_col[:, i : i + 1],
-                slots(ra_bank, X_SHARE, J), ALU.mult, ALU.mult,
+                by_slot(rounded[:, share:]), by_slot(on_s[:]), fkr_col[:, i : i + 1],
+                slots(ra_bank, share, J), ALU.mult, ALU.mult,
             )
-            turn(rounded, bank_part)
+            turn(rounded, x_bank[i])
 
-        for bank, group in zip(x_bank, X_GROUPS):
-            for place, i in enumerate(group):
-                x_front(i, bank[:, place])
-
-        g_grouped = placed([P, N * PACK], BF16, "g_grouped", win_at(1))
+        g_grouped = placed([P, N * PACK], BF16, "g_grouped", win_at(PACK - 1))
         nc.scalar.copy(
             g_grouped[:].bitcast(F32).rearrange("q (p c) -> q p c", c=4),
             g_bank[:].rearrange("q h u p -> q p (h u)"),
         )
-        g_codes, g_plane = quantise(g_grouped, N, "g", picks_at(PACK - 1))
-        for bank, group in zip(x_bank, X_GROUPS):
-            width = len(group) * P
-            grouped = placed([P, width * PACK], BF16, f"x_grouped{group[0]}", win_at(PACK - 1) + 1024 * group[0])
-            nc.scalar.copy(
-                grouped[:].bitcast(F32).rearrange("q (i p u) -> q i p u", u=2, p=P),
-                bank[:].rearrange("q i u p -> q i p u"),
+        x_grouped = {}
+        for i, copy_out, at in (
+            (2, nc.vector.tensor_copy, picks_at(PACK - 1)),
+            (0, nc.scalar.copy, win_at(PACK - 1) + 2048),
+            (1, nc.scalar.copy, win_at(PACK - 1) + 3072),
+            (3, nc.scalar.copy, win_at(0)),
+        ):
+            x_grouped[i] = placed([P, P * PACK], BF16, f"x_grouped{i}", at)
+            copy_out(
+                x_grouped[i][:].bitcast(F32).rearrange("q (p u) -> q p u", u=2),
+                x_bank[i].rearrange("q u p -> q p u"),
             )
-            codes, plane = quantise(grouped, width, f"x{group[0]}", picks_at(PACK - 1) + N + P * group[0])
-            for place, i in enumerate(group):
-                rows = slice(place * P, (place + 1) * P)
-                for nh in range(2):
-                    cols = slice(nh * P, (nh + 1) * P)
-                    nc.tensor.matmul_mx(
-                        w_bank[nh][:, i, :], lhsT=codes[:, rows].bitcast(E5M2X4), lhsT_scale=plane[:, rows],
-                        rhs=g_codes[:, cols].bitcast(E5M2X4), rhs_scale=g_plane[:, cols],
-                        start=True, stop=True,
-                    )
+        g_codes, g_plane = quantise(g_grouped, N, "g")
+        for i in (0, 2, 1, 3):
+            codes, plane = quantise(x_grouped[i], P, f"x{i}")
+            for nh in range(2):
+                cols = slice(nh * P, (nh + 1) * P)
+                nc.tensor.matmul_mx(
+                    w_bank[nh][:, i, :], lhsT=codes[:].bitcast(E5M2X4), lhsT_scale=plane[:],
+                    rhs=g_codes[:, cols].bitcast(E5M2X4), rhs_scale=g_plane[:, cols],
+                    start=True, stop=True,
+                )
 
         old_scaled = placed([P, 2, N], F32, "old_scaled", rounded_at(PACK - 1))
         nc.scalar.activation(old_scaled[:], old_sb[:], COPY, scale=OUT_SCALE)

@@ -20,8 +20,8 @@ COPY = mybir.ActivationFunctionType.Copy
 P = 128
 PACK = 4
 PER_COLUMN = 16
-G_SHARE = (256, 128)
-X_SHARE = (160, 160, 160, 192)
+G_SHARE = (256, 160)
+X_SHARE = (256, 256, 256, 256)
 OUT_SCALE = 0.05
 
 
@@ -151,14 +151,14 @@ def tile_list_directions_headpicks_bounded_larger_kernel(
             rounded = placed([P, J], BF16, f"x_rounded{i}", rounded_at(i))
             nc.scalar.activation(on_s[:], listed(x_win[i], x_list, share, J), COPY)
             nc.vector.tensor_tensor(on_v[:], listed(x_win[i], x_list, 0, share), ra_row[:, :share], ALU.mult)
-            nc.vector.tensor_scalar(rounded[:, :share], on_v[:], fkr_col[:, i : i + 1], None, ALU.mult)
+            nc.scalar.activation(rounded[:, :share], on_v[:], COPY, scale=fkr_col[:, i : i + 1])
             nc.vector.scalar_tensor_tensor(
                 by_slot(rounded[:, share:]), by_slot(on_s[:]), fkr_col[:, i : i + 1],
                 slots(ra_bank, share, J), ALU.mult, ALU.mult,
             )
             turn(rounded, x_bank[i])
 
-        g_grouped = placed([P, N * PACK], BF16, "g_grouped", win_at(PACK - 1))
+        g_grouped = placed([P, N * PACK], BF16, "g_grouped", win_at(0))
         nc.scalar.copy(
             g_grouped[:].bitcast(F32).rearrange("q (p c) -> q p c", c=4),
             g_bank[:].rearrange("q h u p -> q p (h u)"),
@@ -166,9 +166,9 @@ def tile_list_directions_headpicks_bounded_larger_kernel(
         x_grouped = {}
         for i, copy_out, at in (
             (2, nc.vector.tensor_copy, picks_at(PACK - 1)),
-            (0, nc.scalar.copy, win_at(PACK - 1) + 2048),
-            (1, nc.scalar.copy, win_at(PACK - 1) + 3072),
-            (3, nc.scalar.copy, win_at(0)),
+            (0, nc.scalar.copy, win_at(PACK - 1)),
+            (1, nc.scalar.copy, win_at(PACK - 1) + 1024),
+            (3, nc.scalar.copy, win_at(PACK - 1) + 3072),
         ):
             x_grouped[i] = placed([P, P * PACK], BF16, f"x_grouped{i}", at)
             copy_out(
@@ -189,7 +189,7 @@ def tile_list_directions_headpicks_bounded_larger_kernel(
         old_scaled = placed([P, 2, N], F32, "old_scaled", rounded_at(PACK - 1))
         nc.scalar.activation(old_scaled[:], old_sb[:], COPY, scale=OUT_SCALE)
         w_grouped = [keep.tile([P, P * PACK], BF16, name=f"w_grouped{nh}", align_bytes=64) for nh in range(2)]
-        for nh, copy_out in enumerate((nc.vector.tensor_copy, nc.scalar.copy)):
+        for nh, copy_out in enumerate((nc.scalar.copy, nc.vector.tensor_copy)):
             copy_out(
                 w_grouped[nh][:].rearrange("p (n i) -> p n i", i=PACK),
                 w_bank[nh][:].rearrange("p i n -> p n i"),

from contextlib import ExitStack

import concourse.mybir as mybir
from concourse.masks import make_identity

K, J, N, R, T, V = 512, 512, 256, 256, 1024, 1024
FLOPS = 2 * J * K * N + 2 * K * R * N

F32 = mybir.dt.float32
BF16 = mybir.dt.bfloat16
I32 = mybir.dt.int32
U32 = mybir.dt.uint32
U16 = mybir.dt.uint16
U8 = mybir.dt.uint8
E5M2X4 = mybir.dt.float8_e5m2_x4
E2M1X4 = mybir.dt.float4_e2m1fn_x4
ALU = mybir.AluOpType
COPY = mybir.ActivationFunctionType.Copy

P = 128
PACK = 4
PER_COLUMN = 16
G_SHARE = (256, 160)
X_SHARE = (256, 256, 256, 256)
OUT_SCALE = 0.05


def tile_list_directions_headpicks_bounded_larger_kernel(
    tc, xf, ra, gt, rb, cp, fkr, dr_words, dr_scales, old, offs, offs2, out
):
    nc = tc.nc
    with ExitStack() as ctx:
        lists = ctx.enter_context(tc.tile_pool(name="lists", bufs=1))
        keep = ctx.enter_context(tc.tile_pool(name="keep", bufs=1))
        shared = ctx.enter_context(tc.tile_pool(name="shared", bufs=1))
        psum = ctx.enter_context(tc.psum_pool(name="psum", bufs=1))

        g_list = lists.tile([P, J // PER_COLUMN], U16, name="g_list")
        x_list = lists.tile([P, J // PER_COLUMN], U16, name="x_list")
        g_rows = gt.rearrange("(p h) v -> h p v", h=2)
        x_rows = xf.rearrange("(p i) t -> i p t", i=PACK)

        def placed(shape, dtype, name, offset):
            return shared.tile(shape, dtype, name=name, offset=offset, align_bytes=64)

        def win_at(i):
            return 4096 * i

        def picks_at(i):
            return 4096 * PACK + 2048 * (i + 2)

        def rounded_at(i):
            return 6144 * PACK + 2048 * (i + 2)

        g_win = [keep.tile([P, V], F32, name=f"g_win{h}") for h in range(2)]
        x_win = [placed([P, T], F32, f"x_win{i}", win_at(i)) for i in range(PACK)]
        rb_col = keep.tile([P, PACK], F32, name="rb_col")
        ra_col = keep.tile([P, PACK], F32, name="ra_col")
        fkr_col = keep.tile([P, PACK], F32, name="fkr_col")
        cp_col = keep.tile([P, 2], F32, name="cp_col")

        nc.sync.dma_start(rb_col[:], rb.rearrange("o (q t) -> q (o t)", t=PACK))
        nc.sync.dma_start(g_win[0][:], g_rows[0])
        nc.sync.dma_start(g_list[:], offs2)
        nc.sync.dma_start(cp_col[:], cp.rearrange("(p h) o -> p (h o)", h=2))
        nc.sync.dma_start(ra_col[:], ra.rearrange("o (q t) -> q (o t)", t=PACK))
        nc.sync.dma_start(x_list[:], offs)
        nc.sync.dma_start(fkr_col[:], fkr.rearrange("o (p i) -> p (o i)", i=PACK))
        nc.sync.dma_start(g_win[1][:], g_rows[1])
        for i in range(PACK):
            nc.sync.dma_start(x_win[i][:], x_rows[i])

        old_sb = keep.tile([P, 2, N], F32, name="old_sb")
        nc.sync.dma_start(old_sb[:], old.rearrange("(h p) n -> p h n", p=P))
        dr_codes = keep.tile([P, 2 * R], U8, name="dr_codes", align_bytes=64)
        nc.sync.dma_start(dr_codes[:].bitcast(I32), dr_words[0].bitcast(I32))
        dr_plane = keep.tile([P, R], U8, name="dr_plane", align_bytes=64)
        nc.gpsimd.memset(dr_plane[:].bitcast(I32), 0)
        for quad in range(4):
            nc.sync.dma_start(
                dr_plane[32 * quad : 32 * quad + 4, :].bitcast(I32),
                dr_scales[0, 4 * quad : 4 * quad + 4, :].bitcast(I32),
            )

        warm = keep.tile([P, 2], F32, name="warm")
        nc.vector.memset(warm[:, 0:1], 0.0)
        nc.scalar.activation(warm[:, 1:2], warm[:, 0:1], COPY)

        ident = keep.tile([P, P], F32, name="ident")
        make_identity(nc, ident[:])

        def spread(col, tag):
            bank = psum.tile([P, PACK, P], F32, name=tag + "_spread", tag=tag)
            for t in range(PACK):
                nc.tensor.transpose(bank[:, t, :], col[:, t : t + 1].to_broadcast([P, P]), ident[:])
            return bank

        def by_slot(ap):
            return ap.rearrange("p (q t) -> p q t", t=PACK)

        def slots(bank, j0, j1):
            return bank[:, :, j0 // PACK : j1 // PACK].rearrange("p t q -> p q t")

        def listed(win, lst, j0, j1):
            return win[:].indirect(lst[:, j0 // PER_COLUMN : j1 // PER_COLUMN])

        rb_bank = spread(rb_col, "bank_a")
        ra_bank = spread(ra_col, "bank_ra")
        ra_row = keep.tile([P, max(X_SHARE)], F32, name="ra_row")
        nc.scalar.activation(by_slot(ra_row[:]), slots(ra_bank, 0, max(X_SHARE)), COPY)

        def turn(rounded, bank_part):
            words = rounded[:].bitcast(F32)
            for u in range(2):
                nc.tensor.transpose(bank_part[:, u, :], words[:, u::2], ident[:])

        def quantise(grouped, width, name, plane_at=None):
            codes = keep.tile([P, width], U32, name=name + "_codes", align_bytes=64)
            if plane_at is None:
                plane = keep.tile([P, width], U8, name=name + "_plane", align_bytes=64)
            else:
                plane = placed([P, width], U8, name + "_plane", plane_at)
            nc.vector.quantize_mx(codes[:].bitcast(E5M2X4), plane[:], grouped[:])
            return codes, plane

        g_bank = psum.tile([P, 2, 2, P], F32, name="g_bank", tag="bank_b")
        for h in range(2):
            share = G_SHARE[h]
            on_v = keep.tile([P, share], F32, name=f"g_on_v{h}")
            on_s = placed([P, J - share], F32, f"g_on_s{h}", picks_at(h - 2))
            rounded = keep.tile([P, J], BF16, name=f"g_rounded{h}")
            nc.scalar.activation(on_s[:], listed(g_win[h], g_list, share, J), COPY)
            nc.vector.tensor_copy(on_v[:], listed(g_win[h], g_list, 0, share))
            for part, j0, j1 in ((on_v, 0, share), (on_s, share, J)):
                nc.vector.scalar_tensor_tensor(
                    by_slot(rounded[:, j0:j1]), by_slot(part[:]), cp_col[:, h : h + 1],
                    slots(rb_bank, j0, j1), ALU.min, ALU.mult,
                )
            turn(rounded, g_bank[:, h])

        w_bank = [psum.tile([P, PACK, P], F32, name=f"w_bank{nh}", tag=f"bank_w{nh}") for nh in range(2)]
        x_pair = psum.tile([P, 2, 2, P], F32, name="x_pair", tag="bank_x0")
        x_bank = [x_pair[:, 0], x_pair[:, 1]] + [
            psum.tile([P, 2, P], F32, name=f"x_bank{i}", tag=f"bank_x{i}")[:] for i in range(2, PACK)
        ]

        for i in range(PACK):
            share = X_SHARE[i]
            on_v = placed([P, share], F32, f"x_on_v{i}", picks_at(i - 2))
            on_s = placed([P, J - share], F32, f"x_on_s{i}", picks_at(i))
            rounded = placed([P, J], BF16, f"x_rounded{i}", rounded_at(i))
            nc.scalar.activation(on_s[:], listed(x_win[i], x_list, share, J), COPY)
            nc.vector.tensor_tensor(on_v[:], listed(x_win[i], x_list, 0, share), ra_row[:, :share], ALU.mult)
            nc.scalar.activation(rounded[:, :share], on_v[:], COPY, scale=fkr_col[:, i : i + 1])
            nc.vector.scalar_tensor_tensor(
                by_slot(rounded[:, share:]), by_slot(on_s[:]), fkr_col[:, i : i + 1],
                slots(ra_bank, share, J), ALU.mult, ALU.mult,
            )
            turn(rounded, x_bank[i])

        g_grouped = placed([P, N * PACK], BF16, "g_grouped", win_at(0))
        nc.scalar.copy(
            g_grouped[:].bitcast(F32).rearrange("q (p c) -> q p c", c=4),
            g_bank[:].rearrange("q h u p -> q p (h u)"),
        )
        x_grouped = {}
        for i, copy_out, at in (
            (2, nc.vector.tensor_copy, picks_at(PACK - 1)),
            (0, nc.scalar.copy, win_at(PACK - 1)),
            (1, nc.scalar.copy, win_at(PACK - 1) + 1024),
            (3, nc.scalar.copy, win_at(PACK - 1) + 3072),
        ):
            x_grouped[i] = placed([P, P * PACK], BF16, f"x_grouped{i}", at)
            copy_out(
                x_grouped[i][:].bitcast(F32).rearrange("q (p u) -> q p u", u=2),
                x_bank[i].rearrange("q u p -> q p u"),
            )
        g_codes, g_plane = quantise(g_grouped, N, "g")
        for i in (0, 2, 1, 3):
            codes, plane = quantise(x_grouped[i], P, f"x{i}")
            for nh in range(2):
                cols = slice(nh * P, (nh + 1) * P)
                nc.tensor.matmul_mx(
                    w_bank[nh][:, i, :], lhsT=codes[:].bitcast(E5M2X4), lhsT_scale=plane[:],
                    rhs=g_codes[:, cols].bitcast(E5M2X4), rhs_scale=g_plane[:, cols],
                    start=True, stop=True,
                )

        old_scaled = placed([P, 2, N], F32, "old_scaled", rounded_at(PACK - 1))
        nc.scalar.activation(old_scaled[:], old_sb[:], COPY, scale=OUT_SCALE)
        w_grouped = [keep.tile([P, P * PACK], BF16, name=f"w_grouped{nh}", align_bytes=64) for nh in range(2)]
        for nh, copy_out in enumerate((nc.scalar.copy, nc.vector.tensor_copy)):
            copy_out(
                w_grouped[nh][:].rearrange("p (n i) -> p n i", i=PACK),
                w_bank[nh][:].rearrange("p i n -> p n i"),
            )
        w_mx = [quantise(w_grouped[nh], P, f"w{nh}") for nh in range(2)]
        out_rows = out.rearrange("(h p) n -> p h n", p=P)
        for nh, tag in enumerate(("bank_a", "bank_b")):
            codes, plane = w_mx[nh]
            cols = slice(nh * P, (nh + 1) * P)
            v_bank = psum.tile([P, 2, P], F32, name=f"v_bank{nh}", tag=tag)
            for rh in range(2):
                nc.tensor.matmul_mx(
                    v_bank[:, rh, :],
                    lhsT=dr_codes[:, 2 * rh * P : 2 * (rh + 1) * P].bitcast(E2M1X4),
                    lhsT_scale=dr_plane[:, rh * P : (rh + 1) * P],
                    rhs=codes[:].bitcast(E5M2X4), rhs_scale=plane[:],
                    start=True, stop=True,
                )
            result = keep.tile([P, 2, P], F32, name=f"result{nh}")
            nc.vector.scalar_tensor_tensor(
                result[:], v_bank[:], OUT_SCALE, old_scaled[:, :, cols], ALU.mult, ALU.max
            )
            nc.sync.dma_start(out_rows[:, :, cols], result[:])
